import numpy as np
import ml_dtypes


def mxq(x, axis, fmt="e4m3"):
    dtype, down = {"e4m3": (ml_dtypes.float8_e4m3fn, 7), "e5m2": (ml_dtypes.float8_e5m2, 14)}[fmt]
    v = np.moveaxis(np.asarray(x, np.float32).astype(ml_dtypes.bfloat16).astype(np.float64), axis, -1)
    blocks = v.reshape(v.shape[:-1] + (-1, 32))
    amax = np.abs(blocks).max(-1, keepdims=True)
    byte = np.maximum(np.where(amax > 0, np.frexp(amax)[1] - 1 + 127, 0) - down, 1)
    scale = np.exp2(byte - 127.0)
    codes = (blocks / scale).astype(np.float32).astype(dtype).astype(np.float64)
    return np.moveaxis((codes * scale).reshape(v.shape), -1, axis)


WIDE = False


def mx_kscale(k):
    if not WIDE:
        return np.ones(k)
    levels = np.array([10, -10, 5, -5, 0])
    if k % 512:
        return np.exp2(np.random.permutation(np.resize(levels, k // 32))).repeat(32)
    a = np.empty((k // 512, 16))
    for p in range(k // 512):
        a[p, :8] = np.random.permutation(np.resize(levels, 8))
        for g in range(8):
            far = levels[np.abs(levels - a[p, g]) >= 10]
            a[p, g + 8] = far[np.random.randint(len(far))]
    return np.exp2(a.ravel()).repeat(32)


def f64(x):
    return np.asarray(x).astype(np.float64)


def striped8(idx):
    return np.asarray(idx).reshape(8, -1, 16).transpose(0, 2, 1).reshape(128, -1).astype(np.uint16)


def unstriped8(offs):
    return offs.reshape(8, 16, -1).transpose(0, 2, 1).reshape(8, -1).astype(np.int64)


def pick8(x, idx, run):
    r = np.arange(len(x))
    return x[r[:, None], idx[r % (8 * run) // run]]


E2M1 = np.array([0.0, 0.5, 1.0, 1.5, 2.0, 3.0, 4.0, 6.0, -0.0, -0.5, -1.0, -1.5, -2.0, -3.0, -4.0, -6.0])


def pack_weight(w, fmt):
    k, n = w.shape
    w = f64(np.asarray(w, np.float32).astype(ml_dtypes.bfloat16)).reshape(k // 32, 32, n)
    amax = np.abs(w).max(1)
    if fmt == "e4m3":
        byte = np.frexp(amax)[1] - 1 + 127 - 7
    else:
        mant, ex = np.frexp(amax / 6.0)
        byte = np.where(mant > 0.5, ex, ex - 1) + 127
    byte = np.clip(np.where(amax > 0, byte, 1), 1, 254)
    scaled = (w * np.exp2(127.0 - byte)[:, None, :]).reshape(k, n).astype(np.float32)
    by_word = np.ascontiguousarray(scaled.reshape(k // 512, 128, 4, n).transpose(0, 1, 3, 2))
    if fmt == "e4m3":
        words = by_word.astype(ml_dtypes.float8_e4m3fn).view(np.uint8)
    else:
        c = by_word.astype(ml_dtypes.float4_e2m1fn).view(np.uint8) & 0xF
        words = (c[..., 0::2] | (c[..., 1::2] << 4)).reshape(k // 512, 128, 2 * n)
    return np.ascontiguousarray(words), np.ascontiguousarray(byte.astype(np.uint8).reshape(k // 512, 16, n))


def unpack_weight(words, scales, fmt):
    g, _, n = scales.shape
    words = np.ascontiguousarray(words).reshape(g, 128, n, -1)
    if fmt == "e4m3":
        vals = words.view(ml_dtypes.float8_e4m3fn).astype(np.float64)
    else:
        nib = np.empty((g, 128, n, 4), np.uint8)
        nib[..., 0::2] = words & 0xF
        nib[..., 1::2] = words >> 4
        vals = E2M1[nib]
    vals = vals * np.repeat(np.exp2(scales.astype(np.float64) - 127.0), 8, axis=1)[..., None]
    return vals.transpose(0, 1, 3, 2).reshape(g * 512, n)


D, K, T, U, X, S, I, Q = 512, 512, 1024, 1024, 1024, 1024, 512, 128


def setup_inputs():
    n = np.random.standard_normal
    idx = np.stack([np.random.permutation(T)[:I] for _ in range(8)])
    idx2 = np.stack([np.random.permutation(U)[:I] for _ in range(8)])
    idx3 = np.stack([np.random.permutation(X)[:I] for _ in range(8)])
    idx4 = np.stack([np.random.permutation(S)[:I] for _ in range(8)])
    idx5 = np.stack([np.random.permutation(X)[:I] for _ in range(8)])
    idx6 = np.stack([np.random.permutation(S)[:I] for _ in range(8)])
    fd = mx_kscale(D)
    fk = mx_kscale(K)
    wqp = pack_weight(n((D, K)) * 1.0 / np.sqrt(D) * fd[:, None] * fk, "e4m3")
    keysp = pack_weight(n((K, T)) * 1.0 / np.sqrt(K) / fk[:, None], "e4m3")
    notesp = pack_weight(n((K, U)) * 1.0 / np.sqrt(K) / fk[:, None], "e2m1")
    usersp = pack_weight(n((D, X)) * 1.0 / np.sqrt(D) * fd[:, None], "e4m3")
    shelvesp = pack_weight(n((D, S)) * 1.0 / np.sqrt(D) * fd[:, None], "e2m1")
    return {
        "states": (n((D, Q)) * 0.95 / fd[:, None]).astype(np.float32),
        "wq_words": wqp[0],
        "wq_scales": wqp[1],
        "keys_words": keysp[0],
        "keys_scales": keysp[1],
        "notes_words": notesp[0],
        "notes_scales": notesp[1],
        "users_words": usersp[0],
        "users_scales": usersp[1],
        "shelves_words": shelvesp[0],
        "shelves_scales": shelvesp[1],
        "offs": striped8(idx),
        "offs2": striped8(idx2),
        "offs3": striped8(idx3),
        "offs4": striped8(idx4),
        "offs5": striped8(idx5),
        "offs6": striped8(idx6),
    }


def reference(states, wq_words, wq_scales, keys_words, keys_scales, notes_words, notes_scales, users_words, users_scales, shelves_words, shelves_scales, offs, offs2, offs3, offs4, offs5, offs6):
    idx = unstriped8(offs)
    idx2 = unstriped8(offs2)
    idx3 = unstriped8(offs3)
    idx4 = unstriped8(offs4)
    idx5 = unstriped8(offs5)
    idx6 = unstriped8(offs6)
    wqu = unpack_weight(wq_words, wq_scales, "e4m3")
    keysu = unpack_weight(keys_words, keys_scales, "e4m3")
    notesu = unpack_weight(notes_words, notes_scales, "e2m1")
    usersu = unpack_weight(users_words, users_scales, "e4m3")
    shelvesu = unpack_weight(shelves_words, shelves_scales, "e2m1")
    statesq = mxq(f64(states), 0, "e4m3")
    qv = wqu.T @ statesq
    qvq = mxq(qv, 0, "e4m3")
    a = qvq.T @ keysu
    b = qvq.T @ notesu
    c0 = statesq.T @ usersu
    d0 = statesq.T @ shelvesu
    r = pick8(a, idx, 16) - pick8(b, idx2, 16)
    f1 = np.zeros((Q, X))
    f1[np.arange(Q)[:, None], idx3[np.arange(Q) % 128 // 16]] = r
    f2 = np.zeros((Q, S))
    f2[np.arange(Q)[:, None], idx4[np.arange(Q) % 128 // 16]] = r
    cc = c0 + f1
    dd = d0 - f2
    y = pick8(cc, idx5, 16) - pick8(dd, idx6, 16)
    return y

@@ -1,0 +1,176 @@
+from contextlib import ExitStack
+
+import concourse.mybir as mybir
+
+F32 = mybir.dt.float32
+BF16 = mybir.dt.bfloat16
+I32 = mybir.dt.int32
+U32 = mybir.dt.uint32
+U16 = mybir.dt.uint16
+U8 = mybir.dt.uint8
+FP8X4 = mybir.dt.float8_e4m3fn_x4
+FP4X4 = mybir.dt.float4_e2m1fn_x4
+ADD = mybir.AluOpType.add
+SUB = mybir.AluOpType.subtract
+COPY = mybir.ActivationFunctionType.Copy
+
+P = 128
+PACK = 4
+Q = 128
+K = 512
+COLS = 1024
+BANK = 512
+SLOTS = 512
+HALF = SLOTS // 2
+LIST_COLS = SLOTS // 16
+POOL_COLS = 288
+
+FLOPS = 2 * 512 * 512 * 128 + 4 * 2 * 512 * 128 * 1024
+
+
+def tile_attend_audit_madefour_kernel(tc, states, wq_words, wq_scales, keys_words, keys_scales, notes_words,
+                                       notes_scales, users_words, users_scales, shelves_words, shelves_scales,
+                                       offs, offs2, offs3, offs4, offs5, offs6, out):
+    nc = tc.nc
+    with ExitStack() as ctx:
+        lists = ctx.enter_context(tc.tile_pool(name="lists", bufs=1))
+        keep = ctx.enter_context(tc.tile_pool(name="keep", bufs=1))
+        psum = ctx.enter_context(tc.psum_pool(name="psum", bufs=1))
+
+        def load_words(queue, tile, words):
+            queue.dma_start(out=tile[:].bitcast(I32), in_=words.bitcast(I32))
+
+        def load_scales(queue, plane, first, scales):
+            for quad in range(4):
+                row = 32 * quad + first
+                queue.dma_start(out=plane[row:row + 4, :].bitcast(I32),
+                                in_=scales[0, 4 * quad:4 * quad + 4, :].bitcast(I32))
+
+        def load_list(name, src):
+            tile = lists.tile([P, LIST_COLS], U16, name=name)
+            nc.sync.dma_start(tile[:], src)
+            return tile
+
+        def half(offsets, h):
+            return offsets[:, h * LIST_COLS // 2:(h + 1) * LIST_COLS // 2]
+
+        wq_plane_raw = keep.tile([P, K], U8, align_bytes=64)
+        notes_plane = keep.tile([P, COLS], U8, align_bytes=64)
+        keys_plane = keep.tile([P, COLS], U8, align_bytes=64)
+        shelves_plane = keep.tile([P, COLS], U8, align_bytes=64)
+        users_plane = keep.tile([P, COLS], U8, align_bytes=64)
+        for plane in (wq_plane_raw, notes_plane, keys_plane, shelves_plane, users_plane):
+            nc.vector.memset(plane[:].bitcast(U32), 0)
+        f1 = keep.tile([P, COLS], F32)
+        f2 = keep.tile([P, COLS], F32)
+        nc.vector.memset(f2[:], 0.0)
+        nc.vector.memset(f1[:], 0.0)
+
+        states_raw = keep.tile([P, PACK, Q], F32, align_bytes=64)
+        nc.sync.dma_start(out=states_raw[:], in_=states.rearrange("(p j) q -> p j q", j=PACK))
+        load_scales(nc.sync, wq_plane_raw, 12, wq_scales)
+        wq_raw = keep.tile([P, K], U32, align_bytes=64)
+        load_words(nc.sync, wq_raw, wq_words[0].rearrange("p n t -> p (n t)"))
+        notes = keep.tile([P, 2 * COLS], U8, align_bytes=64)
+        load_words(nc.sync, notes, notes_words[0])
+        load_scales(nc.sync, notes_plane, 0, notes_scales)
+        keys = keep.tile([P, COLS], U32, align_bytes=64)
+        load_words(nc.sync, keys, keys_words[0].rearrange("p n t -> p (n t)"))
+        load_scales(nc.sync, keys_plane, 4, keys_scales)
+        idx2 = load_list("idx2", offs2)
+        idx = load_list("idx", offs)
+        idx4 = load_list("idx4", offs4)
+        shelves = keep.tile([P, 2 * COLS], U8, align_bytes=64)
+        load_words(nc.sync, shelves, shelves_words[0])
+        load_scales(nc.sync, shelves_plane, 0, shelves_scales)
+        idx3 = load_list("idx3", offs3)
+        users = keep.tile([P, COLS], U32, align_bytes=64)
+        load_words(nc.sync, users, users_words[0].rearrange("p n t -> p (n t)"))
+        load_scales(nc.sync, users_plane, 8, users_scales)
+        idx6 = load_list("idx6", offs6)
+        idx5 = load_list("idx5", offs5)
+
+        states_bf = keep.tile([P, Q, PACK], BF16, align_bytes=64)
+        nc.scalar.activation(states_bf[:], states_raw[:].rearrange("p j q -> p q j"), COPY)
+        wq_plane = keep.tile([P, K], U8, align_bytes=64)
+        nc.vector.tensor_copy(out=wq_plane[:].rearrange("p (t c i) -> p c t i", t=PACK, i=16),
+                              in_=wq_plane_raw[:].rearrange("p (c i t) -> p c t i", t=PACK, i=16))
+        sq = keep.tile([P, Q], U32, align_bytes=64)
+        sq_plane = keep.tile([P, Q], U8, align_bytes=64)
+        nc.vector.quantize_mx(out=sq[:].bitcast(FP8X4), scales=sq_plane[:],
+                              in_=states_bf[:].rearrange("p q j -> p (q j)"))
+        wq = [keep.tile([P, 2, P], U32, align_bytes=64, name="wq%d" % u) for u in range(2)]
+        wq_by_place = wq_raw[:].rearrange("p (c i t) -> p c t i", t=PACK, i=4)
+        nc.scalar.copy(wq[0][:].rearrange("p t (c i) -> p c t i", i=4), wq_by_place[:, :, 0:2, :])
+        nc.vector.tensor_copy(out=wq[1][:].bitcast(I32).rearrange("p t (c i) -> p c t i", i=4),
+                              in_=wq_raw[:].bitcast(I32).rearrange("p (c i t) -> p c t i", t=PACK, i=4)[:, :, 2:4, :])
+
+        qv_ps = psum.tile([P, PACK, Q], F32, tag="qv_then_c")
+        for t in range(PACK):
+            cols = slice(t * P, (t + 1) * P)
+            nc.tensor.matmul_mx(out=qv_ps[:, t, :], lhsT=wq[t // 2][:, t % 2, :].bitcast(FP8X4), lhsT_scale=wq_plane[12:P, cols],
+                                rhs=sq[:].bitcast(FP8X4), rhs_scale=sq_plane[:], start=True, stop=True)
+        qv_bf = keep.tile([P, Q, PACK], BF16, align_bytes=64)
+        nc.scalar.activation(qv_bf[:], qv_ps[:].rearrange("p t q -> p q t"), COPY)
+        qq = keep.tile([P, Q], U32, align_bytes=64)
+        qq_plane = keep.tile([P, Q], U8, align_bytes=64)
+        nc.vector.quantize_mx(out=qq[:].bitcast(FP8X4), scales=qq_plane[:],
+                              in_=qv_bf[:].rearrange("p q j -> p (q j)"))
+
+        def scores(tag, h, codes, plane, words, words_plane, first, fp4):
+            bank = psum.tile([P, BANK], F32, tag=tag, name=tag)
+            cols = slice(h * BANK, (h + 1) * BANK)
+            if fp4:
+                moving = words[:, 2 * h * BANK:2 * (h + 1) * BANK].bitcast(FP4X4)
+            else:
+                moving = words[:, cols].bitcast(FP8X4)
+            nc.tensor.matmul_mx(out=bank[:], lhsT=codes[:].bitcast(FP8X4), lhsT_scale=plane[:],
+                                rhs=moving, rhs_scale=words_plane[first:P, cols], start=True, stop=True)
+            return bank
+
+        a = keep.tile([P, COLS], F32)
+        b = keep.tile([P, COLS], F32)
+        for h in range(2):
+            bank = scores("b%d" % h, h, qq, qq_plane, notes, notes_plane, 0, True)
+            nc.scalar.activation(b[:, h * BANK:(h + 1) * BANK], bank[:], COPY)
+        for h in range(2):
+            bank = scores("a%d" % h, h, qq, qq_plane, keys, keys_plane, 4, False)
+            nc.vector.tensor_copy(out=a[:, h * BANK:(h + 1) * BANK], in_=bank[:])
+        d0 = [scores("d%d" % h, h, sq, sq_plane, shelves, shelves_plane, 0, True) for h in range(2)]
+        c0 = [scores(tag, h, sq, sq_plane, users, users_plane, 8, False) for h, tag in enumerate(("c0", "qv_then_c"))]
+
+        gb = [keep.tile([P, HALF], F32, name="gb%d" % h) for h in range(2)]
+        ga1 = keep.tile([P, HALF], F32)
+        r = keep.tile([P, SLOTS], F32)
+        nc.scalar.activation(gb[0][:], b[:].indirect(half(idx2, 0)), COPY)
+        nc.vector.tensor_tensor(r[:, :HALF], a[:].indirect(half(idx, 0)), gb[0][:], SUB)
+        nc.scalar.activation(gb[1][:], b[:].indirect(half(idx2, 1)), COPY)
+        nc.scalar.activation(ga1[:], a[:].indirect(half(idx, 1)), COPY)
+        nc.gpsimd.tensor_tensor(r[:, HALF:], ga1[:], gb[1][:], SUB)
+
+        d0_sb = keep.tile([P, COLS], F32)
+        for h in range(2):
+            nc.scalar.activation(d0_sb[:, h * BANK:(h + 1) * BANK], d0[h][:], COPY)
+        c0_tail = keep.tile([P, POOL_COLS], F32)
+        nc.scalar.activation(c0_tail[:], c0[1][:, BANK - POOL_COLS:], COPY)
+
+        for h in range(2):
+            nc.vector.tensor_copy(f2[:].indirect(half(idx4, h)), r[:, h * HALF:(h + 1) * HALF])
+        nc.vector.tensor_copy(f1[:].indirect(idx3[:]), r[:])
+        dd = keep.tile([P, COLS], F32)
+        nc.gpsimd.tensor_tensor(dd[:], d0_sb[:], f2[:], SUB)
+        gdd = keep.tile([P, SLOTS], F32)
+        nc.scalar.activation(gdd[:], dd[:].indirect(idx6[:]), COPY)
+        cc = keep.tile([P, COLS], F32)
+        split = COLS - POOL_COLS
+        nc.gpsimd.tensor_tensor(cc[:, split:], c0_tail[:], f1[:, split:], ADD)
+        nc.vector.tensor_tensor(cc[:, :BANK], c0[0][:], f1[:, :BANK], ADD)
+        nc.vector.tensor_tensor(cc[:, BANK:split], c0[1][:, :split - BANK], f1[:, BANK:split], ADD)
+
+        y = [keep.tile([P, HALF], F32, name="y%d" % h) for h in range(2)]
+        gcc = keep.tile([P, HALF], F32)
+        nc.vector.tensor_tensor(y[0][:], cc[:].indirect(half(idx5, 0)), gdd[:, :HALF], SUB)
+        nc.sync.dma_start(out=out[:, :HALF], in_=y[0][:])
+        nc.scalar.activation(gcc[:], cc[:].indirect(half(idx5, 1)), COPY)
+        nc.vector.tensor_tensor(y[1][:], gcc[:], gdd[:, HALF:], SUB)
+        nc.scalar.dma_start(out=out[:, HALF:], in_=y[1][:])

@@ -80,13 +80,13 @@ def tile_attend_audit_madefour_kernel(tc, states, wq_words, wq_scales, keys_word
         idx2 = load_list("idx2", offs2)
         idx = load_list("idx", offs)
         idx4 = load_list("idx4", offs4)
-        shelves = keep.tile([P, 2 * COLS], U8, align_bytes=64)
-        load_words(nc.sync, shelves, shelves_words[0])
-        load_scales(nc.sync, shelves_plane, 0, shelves_scales)
-        idx3 = load_list("idx3", offs3)
         users = keep.tile([P, COLS], U32, align_bytes=64)
         load_words(nc.sync, users, users_words[0].rearrange("p n t -> p (n t)"))
         load_scales(nc.sync, users_plane, 8, users_scales)
+        idx3 = load_list("idx3", offs3)
+        shelves = keep.tile([P, 2 * COLS], U8, align_bytes=64)
+        load_words(nc.sync, shelves, shelves_words[0])
+        load_scales(nc.sync, shelves_plane, 0, shelves_scales)
         idx6 = load_list("idx6", offs6)
         idx5 = load_list("idx5", offs5)
 
@@ -100,10 +100,10 @@ def tile_attend_audit_madefour_kernel(tc, states, wq_words, wq_scales, keys_word
         nc.vector.quantize_mx(out=sq[:].bitcast(FP8X4), scales=sq_plane[:],
                               in_=states_bf[:].rearrange("p q j -> p (q j)"))
         wq = [keep.tile([P, 2, P], U32, align_bytes=64, name="wq%d" % u) for u in range(2)]
-        wq_by_place = wq_raw[:].rearrange("p (c i t) -> p c t i", t=PACK, i=4)
-        nc.scalar.copy(wq[0][:].rearrange("p t (c i) -> p c t i", i=4), wq_by_place[:, :, 0:2, :])
-        nc.vector.tensor_copy(out=wq[1][:].bitcast(I32).rearrange("p t (c i) -> p c t i", i=4),
-                              in_=wq_raw[:].bitcast(I32).rearrange("p (c i t) -> p c t i", t=PACK, i=4)[:, :, 2:4, :])
+        nc.scalar.copy(wq[0][:].rearrange("p t m -> p m t"),
+                       wq_raw[:].rearrange("p (m t) -> p m t", t=PACK)[:, :, 0:2])
+        nc.vector.tensor_copy(out=wq[1][:].bitcast(I32).rearrange("p t m -> p m t"),
+                              in_=wq_raw[:].bitcast(I32).rearrange("p (m t) -> p m t", t=PACK)[:, :, 2:4])
 
         qv_ps = psum.tile([P, PACK, Q], F32, tag="qv_then_c")
         for t in range(PACK):
@@ -117,42 +117,45 @@ def tile_attend_audit_madefour_kernel(tc, states, wq_words, wq_scales, keys_word
         nc.vector.quantize_mx(out=qq[:].bitcast(FP8X4), scales=qq_plane[:],
                               in_=qv_bf[:].rearrange("p q j -> p (q j)"))
 
-        def scores(tag, h, codes, plane, words, words_plane, first, fp4):
-            bank = psum.tile([P, BANK], F32, tag=tag, name=tag)
-            cols = slice(h * BANK, (h + 1) * BANK)
+        def scores(tag, lo, hi, codes, plane, words, words_plane, first, fp4):
+            bank = psum.tile([P, hi - lo], F32, tag=tag, name=tag)
             if fp4:
-                moving = words[:, 2 * h * BANK:2 * (h + 1) * BANK].bitcast(FP4X4)
+                moving = words[:, 2 * lo:2 * hi].bitcast(FP4X4)
             else:
-                moving = words[:, cols].bitcast(FP8X4)
+                moving = words[:, lo:hi].bitcast(FP8X4)
             nc.tensor.matmul_mx(out=bank[:], lhsT=codes[:].bitcast(FP8X4), lhsT_scale=plane[:],
-                                rhs=moving, rhs_scale=words_plane[first:P, cols], start=True, stop=True)
+                                rhs=moving, rhs_scale=words_plane[first:P, lo:hi], start=True, stop=True)
             return bank
 
         a = keep.tile([P, COLS], F32)
         b = keep.tile([P, COLS], F32)
         for h in range(2):
-            bank = scores("b%d" % h, h, qq, qq_plane, notes, notes_plane, 0, True)
+            bank = scores("b%d" % h, h * BANK, (h + 1) * BANK, qq, qq_plane, notes, notes_plane, 0, True)
             nc.scalar.activation(b[:, h * BANK:(h + 1) * BANK], bank[:], COPY)
-        for h in range(2):
-            bank = scores("a%d" % h, h, qq, qq_plane, keys, keys_plane, 4, False)
-            nc.vector.tensor_copy(out=a[:, h * BANK:(h + 1) * BANK], in_=bank[:])
-        d0 = [scores("d%d" % h, h, sq, sq_plane, shelves, shelves_plane, 0, True) for h in range(2)]
-        c0 = [scores(tag, h, sq, sq_plane, users, users_plane, 8, False) for h, tag in enumerate(("c0", "qv_then_c"))]
+        a_banks = [scores("a%d" % n, lo, hi, qq, qq_plane, keys, keys_plane, 4, False)
+                   for n, (lo, hi) in enumerate(((0, 512), (512, 768), (768, 1024)))]
+        nc.vector.tensor_copy(out=a[:, 0:512], in_=a_banks[0][:])
+        nc.vector.tensor_copy(out=a[:, 512:768], in_=a_banks[1][:])
+        c0 = [scores(tag, h * BANK, (h + 1) * BANK, sq, sq_plane, users, users_plane, 8, False)
+              for h, tag in enumerate(("c0", "qv_then_c"))]
+        d0 = [scores(tag, h * BANK, (h + 1) * BANK, sq, sq_plane, shelves, shelves_plane, 0, True)
+              for h, tag in enumerate(("d0", "b0"))]
 
         gb = [keep.tile([P, HALF], F32, name="gb%d" % h) for h in range(2)]
         ga1 = keep.tile([P, HALF], F32)
         r = keep.tile([P, SLOTS], F32)
         nc.scalar.activation(gb[0][:], b[:].indirect(half(idx2, 0)), COPY)
+        nc.scalar.activation(a[:, 768:1024], a_banks[2][:], COPY)
         nc.vector.tensor_tensor(r[:, :HALF], a[:].indirect(half(idx, 0)), gb[0][:], SUB)
         nc.scalar.activation(gb[1][:], b[:].indirect(half(idx2, 1)), COPY)
         nc.scalar.activation(ga1[:], a[:].indirect(half(idx, 1)), COPY)
         nc.gpsimd.tensor_tensor(r[:, HALF:], ga1[:], gb[1][:], SUB)
 
-        d0_sb = keep.tile([P, COLS], F32)
-        for h in range(2):
-            nc.scalar.activation(d0_sb[:, h * BANK:(h + 1) * BANK], d0[h][:], COPY)
         c0_tail = keep.tile([P, POOL_COLS], F32)
         nc.scalar.activation(c0_tail[:], c0[1][:, BANK - POOL_COLS:], COPY)
+        d0_sb = keep.tile([P, COLS], F32, tag="d0_then_cc")
+        for h in range(2):
+            nc.scalar.activation(d0_sb[:, h * BANK:(h + 1) * BANK], d0[h][:], COPY)
 
         for h in range(2):
             nc.vector.tensor_copy(f2[:].indirect(half(idx4, h)), r[:, h * HALF:(h + 1) * HALF])
@@ -161,7 +164,7 @@ def tile_attend_audit_madefour_kernel(tc, states, wq_words, wq_scales, keys_word
         nc.gpsimd.tensor_tensor(dd[:], d0_sb[:], f2[:], SUB)
         gdd = keep.tile([P, SLOTS], F32)
         nc.scalar.activation(gdd[:], dd[:].indirect(idx6[:]), COPY)
-        cc = keep.tile([P, COLS], F32)
+        cc = keep.tile([P, COLS], F32, tag="d0_then_cc")
         split = COLS - POOL_COLS
         nc.gpsimd.tensor_tensor(cc[:, split:], c0_tail[:], f1[:, split:], ADD)
         nc.vector.tensor_tensor(cc[:, :BANK], c0[0][:], f1[:, :BANK], ADD)

@@ -129,9 +129,11 @@ def tile_attend_audit_madefour_kernel(tc, states, wq_words, wq_scales, keys_word
 
         a = keep.tile([P, COLS], F32)
         b = keep.tile([P, COLS], F32)
-        for h in range(2):
-            bank = scores("b%d" % h, h * BANK, (h + 1) * BANK, qq, qq_plane, notes, notes_plane, 0, True)
-            nc.scalar.activation(b[:, h * BANK:(h + 1) * BANK], bank[:], COPY)
+        b_banks = [scores("b%d" % n, lo, hi, qq, qq_plane, notes, notes_plane, 0, True)
+                   for n, (lo, hi) in enumerate(((0, 512), (512, 768), (768, 1024)))]
+        nc.scalar.activation(b[:, 0:512], b_banks[0][:], COPY)
+        nc.vector.tensor_copy(out=b[:, 512:768], in_=b_banks[1][:])
+        nc.scalar.activation(b[:, 768:1024], b_banks[2][:], COPY)
         a_banks = [scores("a%d" % n, lo, hi, qq, qq_plane, keys, keys_plane, 4, False)
                    for n, (lo, hi) in enumerate(((0, 512), (512, 768), (768, 1024)))]
         nc.vector.tensor_copy(out=a[:, 0:512], in_=a_banks[0][:])
@@ -139,7 +141,7 @@ def tile_attend_audit_madefour_kernel(tc, states, wq_words, wq_scales, keys_word
         c0 = [scores(tag, h * BANK, (h + 1) * BANK, sq, sq_plane, users, users_plane, 8, False)
               for h, tag in enumerate(("c0", "qv_then_c"))]
         d0 = [scores(tag, h * BANK, (h + 1) * BANK, sq, sq_plane, shelves, shelves_plane, 0, True)
-              for h, tag in enumerate(("d0", "b0"))]
+              for h, tag in enumerate(("b1", "b0"))]
 
         gb = [keep.tile([P, HALF], F32, name="gb%d" % h) for h in range(2)]
         ga1 = keep.tile([P, HALF], F32)

from contextlib import ExitStack

import concourse.mybir as mybir

F32 = mybir.dt.float32
BF16 = mybir.dt.bfloat16
I32 = mybir.dt.int32
U32 = mybir.dt.uint32
U16 = mybir.dt.uint16
U8 = mybir.dt.uint8
FP8X4 = mybir.dt.float8_e4m3fn_x4
FP4X4 = mybir.dt.float4_e2m1fn_x4
ADD = mybir.AluOpType.add
SUB = mybir.AluOpType.subtract
COPY = mybir.ActivationFunctionType.Copy

P = 128
PACK = 4
Q = 128
K = 512
COLS = 1024
BANK = 512
SLOTS = 512
HALF = SLOTS // 2
LIST_COLS = SLOTS // 16
POOL_COLS = 288

FLOPS = 2 * 512 * 512 * 128 + 4 * 2 * 512 * 128 * 1024


def tile_attend_audit_madefour_kernel(tc, states, wq_words, wq_scales, keys_words, keys_scales, notes_words,
                                       notes_scales, users_words, users_scales, shelves_words, shelves_scales,
                                       offs, offs2, offs3, offs4, offs5, offs6, out):
    nc = tc.nc
    with ExitStack() as ctx:
        lists = ctx.enter_context(tc.tile_pool(name="lists", bufs=1))
        keep = ctx.enter_context(tc.tile_pool(name="keep", bufs=1))
        psum = ctx.enter_context(tc.psum_pool(name="psum", bufs=1))

        def load_words(queue, tile, words):
            queue.dma_start(out=tile[:].bitcast(I32), in_=words.bitcast(I32))

        def load_scales(queue, plane, first, scales):
            for quad in range(4):
                row = 32 * quad + first
                queue.dma_start(out=plane[row:row + 4, :].bitcast(I32),
                                in_=scales[0, 4 * quad:4 * quad + 4, :].bitcast(I32))

        def load_list(name, src):
            tile = lists.tile([P, LIST_COLS], U16, name=name)
            nc.sync.dma_start(tile[:], src)
            return tile

        def half(offsets, h):
            return offsets[:, h * LIST_COLS // 2:(h + 1) * LIST_COLS // 2]

        wq_plane_raw = keep.tile([P, K], U8, align_bytes=64)
        notes_plane = keep.tile([P, COLS], U8, align_bytes=64)
        keys_plane = keep.tile([P, COLS], U8, align_bytes=64)
        shelves_plane = keep.tile([P, COLS], U8, align_bytes=64)
        users_plane = keep.tile([P, COLS], U8, align_bytes=64)
        for plane in (wq_plane_raw, notes_plane, keys_plane, shelves_plane, users_plane):
            nc.vector.memset(plane[:].bitcast(U32), 0)
        f1 = keep.tile([P, COLS], F32)
        f2 = keep.tile([P, COLS], F32)
        nc.vector.memset(f2[:], 0.0)
        nc.vector.memset(f1[:], 0.0)

        states_raw = keep.tile([P, PACK, Q], F32, align_bytes=64)
        nc.sync.dma_start(out=states_raw[:], in_=states.rearrange("(p j) q -> p j q", j=PACK))
        load_scales(nc.sync, wq_plane_raw, 12, wq_scales)
        wq_raw = keep.tile([P, K], U32, align_bytes=64)
        load_words(nc.sync, wq_raw, wq_words[0].rearrange("p n t -> p (n t)"))
        notes = keep.tile([P, 2 * COLS], U8, align_bytes=64)
        load_words(nc.sync, notes, notes_words[0])
        load_scales(nc.sync, notes_plane, 0, notes_scales)
        keys = keep.tile([P, COLS], U32, align_bytes=64)
        load_words(nc.sync, keys, keys_words[0].rearrange("p n t -> p (n t)"))
        load_scales(nc.sync, keys_plane, 4, keys_scales)
        idx2 = load_list("idx2", offs2)
        idx = load_list("idx", offs)
        idx4 = load_list("idx4", offs4)
        users = keep.tile([P, COLS], U32, align_bytes=64)
        load_words(nc.sync, users, users_words[0].rearrange("p n t -> p (n t)"))
        load_scales(nc.sync, users_plane, 8, users_scales)
        idx3 = load_list("idx3", offs3)
        shelves = keep.tile([P, 2 * COLS], U8, align_bytes=64)
        load_words(nc.sync, shelves, shelves_words[0])
        load_scales(nc.sync, shelves_plane, 0, shelves_scales)
        idx6 = load_list("idx6", offs6)
        idx5 = load_list("idx5", offs5)

        states_bf = keep.tile([P, Q, PACK], BF16, align_bytes=64)
        nc.scalar.activation(states_bf[:], states_raw[:].rearrange("p j q -> p q j"), COPY)
        wq_plane = keep.tile([P, K], U8, align_bytes=64)
        nc.vector.tensor_copy(out=wq_plane[:].rearrange("p (t c i) -> p c t i", t=PACK, i=16),
                              in_=wq_plane_raw[:].rearrange("p (c i t) -> p c t i", t=PACK, i=16))
        sq = keep.tile([P, Q], U32, align_bytes=64)
        sq_plane = keep.tile([P, Q], U8, align_bytes=64)
        nc.vector.quantize_mx(out=sq[:].bitcast(FP8X4), scales=sq_plane[:],
                              in_=states_bf[:].rearrange("p q j -> p (q j)"))
        wq = [keep.tile([P, 2, P], U32, align_bytes=64, name="wq%d" % u) for u in range(2)]
        nc.scalar.copy(wq[0][:].rearrange("p t m -> p m t"),
                       wq_raw[:].rearrange("p (m t) -> p m t", t=PACK)[:, :, 0:2])
        nc.vector.tensor_copy(out=wq[1][:].bitcast(I32).rearrange("p t m -> p m t"),
                              in_=wq_raw[:].bitcast(I32).rearrange("p (m t) -> p m t", t=PACK)[:, :, 2:4])

        qv_ps = psum.tile([P, PACK, Q], F32, tag="qv_then_c")
        for t in range(PACK):
            cols = slice(t * P, (t + 1) * P)
            nc.tensor.matmul_mx(out=qv_ps[:, t, :], lhsT=wq[t // 2][:, t % 2, :].bitcast(FP8X4), lhsT_scale=wq_plane[12:P, cols],
                                rhs=sq[:].bitcast(FP8X4), rhs_scale=sq_plane[:], start=True, stop=True)
        qv_bf = keep.tile([P, Q, PACK], BF16, align_bytes=64)
        nc.scalar.activation(qv_bf[:], qv_ps[:].rearrange("p t q -> p q t"), COPY)
        qq = keep.tile([P, Q], U32, align_bytes=64)
        qq_plane = keep.tile([P, Q], U8, align_bytes=64)
        nc.vector.quantize_mx(out=qq[:].bitcast(FP8X4), scales=qq_plane[:],
                              in_=qv_bf[:].rearrange("p q j -> p (q j)"))

        def scores(tag, lo, hi, codes, plane, words, words_plane, first, fp4):
            bank = psum.tile([P, hi - lo], F32, tag=tag, name=tag)
            if fp4:
                moving = words[:, 2 * lo:2 * hi].bitcast(FP4X4)
            else:
                moving = words[:, lo:hi].bitcast(FP8X4)
            nc.tensor.matmul_mx(out=bank[:], lhsT=codes[:].bitcast(FP8X4), lhsT_scale=plane[:],
                                rhs=moving, rhs_scale=words_plane[first:P, lo:hi], start=True, stop=True)
            return bank

        a = keep.tile([P, COLS], F32)
        b = keep.tile([P, COLS], F32)
        b_banks = [scores("b%d" % n, lo, hi, qq, qq_plane, notes, notes_plane, 0, True)
                   for n, (lo, hi) in enumerate(((0, 512), (512, 768), (768, 1024)))]
        nc.scalar.activation(b[:, 0:512], b_banks[0][:], COPY)
        nc.vector.tensor_copy(out=b[:, 512:768], in_=b_banks[1][:])
        nc.scalar.activation(b[:, 768:1024], b_banks[2][:], COPY)
        a_banks = [scores("a%d" % n, lo, hi, qq, qq_plane, keys, keys_plane, 4, False)
                   for n, (lo, hi) in enumerate(((0, 512), (512, 768), (768, 1024)))]
        nc.vector.tensor_copy(out=a[:, 0:512], in_=a_banks[0][:])
        nc.vector.tensor_copy(out=a[:, 512:768], in_=a_banks[1][:])
        c0 = [scores(tag, h * BANK, (h + 1) * BANK, sq, sq_plane, users, users_plane, 8, False)
              for h, tag in enumerate(("c0", "qv_then_c"))]
        d0 = [scores(tag, h * BANK, (h + 1) * BANK, sq, sq_plane, shelves, shelves_plane, 0, True)
              for h, tag in enumerate(("b1", "b0"))]

        gb = [keep.tile([P, HALF], F32, name="gb%d" % h) for h in range(2)]
        ga1 = keep.tile([P, HALF], F32)
        r = keep.tile([P, SLOTS], F32)
        nc.scalar.activation(gb[0][:], b[:].indirect(half(idx2, 0)), COPY)
        nc.scalar.activation(a[:, 768:1024], a_banks[2][:], COPY)
        nc.vector.tensor_tensor(r[:, :HALF], a[:].indirect(half(idx, 0)), gb[0][:], SUB)
        nc.scalar.activation(gb[1][:], b[:].indirect(half(idx2, 1)), COPY)
        nc.scalar.activation(ga1[:], a[:].indirect(half(idx, 1)), COPY)
        nc.gpsimd.tensor_tensor(r[:, HALF:], ga1[:], gb[1][:], SUB)

        c0_tail = keep.tile([P, POOL_COLS], F32)
        nc.scalar.activation(c0_tail[:], c0[1][:, BANK - POOL_COLS:], COPY)
        d0_sb = keep.tile([P, COLS], F32, tag="d0_then_cc")
        for h in range(2):
            nc.scalar.activation(d0_sb[:, h * BANK:(h + 1) * BANK], d0[h][:], COPY)

        for h in range(2):
            nc.vector.tensor_copy(f2[:].indirect(half(idx4, h)), r[:, h * HALF:(h + 1) * HALF])
        nc.vector.tensor_copy(f1[:].indirect(idx3[:]), r[:])
        dd = keep.tile([P, COLS], F32)
        nc.gpsimd.tensor_tensor(dd[:], d0_sb[:], f2[:], SUB)
        gdd = keep.tile([P, SLOTS], F32)
        nc.scalar.activation(gdd[:], dd[:].indirect(idx6[:]), COPY)
        cc = keep.tile([P, COLS], F32, tag="d0_then_cc")
        split = COLS - POOL_COLS
        nc.gpsimd.tensor_tensor(cc[:, split:], c0_tail[:], f1[:, split:], ADD)
        nc.vector.tensor_tensor(cc[:, :BANK], c0[0][:], f1[:, :BANK], ADD)
        nc.vector.tensor_tensor(cc[:, BANK:split], c0[1][:, :split - BANK], f1[:, BANK:split], ADD)

        y = [keep.tile([P, HALF], F32, name="y%d" % h) for h in range(2)]
        gcc = keep.tile([P, HALF], F32)
        nc.vector.tensor_tensor(y[0][:], cc[:].indirect(half(idx5, 0)), gdd[:, :HALF], SUB)
        nc.sync.dma_start(out=out[:, :HALF], in_=y[0][:])
        nc.scalar.activation(gcc[:], cc[:].indirect(half(idx5, 1)), COPY)
        nc.vector.tensor_tensor(y[1][:], gcc[:], gdd[:, HALF:], SUB)
        nc.scalar.dma_start(out=out[:, HALF:], in_=y[1][:])
